import numpy as np
import ml_dtypes


def mxq(x, axis, fmt="e4m3"):
    dtype, down = {"e4m3": (ml_dtypes.float8_e4m3fn, 7), "e5m2": (ml_dtypes.float8_e5m2, 14)}[fmt]
    v = np.moveaxis(np.asarray(x, np.float32).astype(ml_dtypes.bfloat16).astype(np.float64), axis, -1)
    blocks = v.reshape(v.shape[:-1] + (-1, 32))
    amax = np.abs(blocks).max(-1, keepdims=True)
    byte = np.maximum(np.where(amax > 0, np.frexp(amax)[1] - 1 + 127, 0) - down, 1)
    scale = np.exp2(byte - 127.0)
    codes = (blocks / scale).astype(np.float32).astype(dtype).astype(np.float64)
    return np.moveaxis((codes * scale).reshape(v.shape), -1, axis)


WIDE = False


def mx_kscale(k):
    if not WIDE:
        return np.ones(k)
    levels = np.array([10, -10, 5, -5, 0])
    if k % 512:
        return np.exp2(np.random.permutation(np.resize(levels, k // 32))).repeat(32)
    a = np.empty((k // 512, 16))
    for p in range(k // 512):
        a[p, :8] = np.random.permutation(np.resize(levels, 8))
        for g in range(8):
            far = levels[np.abs(levels - a[p, g]) >= 10]
            a[p, g + 8] = far[np.random.randint(len(far))]
    return np.exp2(a.ravel()).repeat(32)


def f64(x):
    return np.asarray(x).astype(np.float64)


def striped(idx):
    return np.tile(np.asarray(idx).reshape(-1, 16).T, (8, 1)).astype(np.uint16)


def unstriped(offs):
    return offs[:16].T.reshape(-1).astype(np.int64)


E2M1 = np.array([0.0, 0.5, 1.0, 1.5, 2.0, 3.0, 4.0, 6.0, -0.0, -0.5, -1.0, -1.5, -2.0, -3.0, -4.0, -6.0])


def pack_weight(w, fmt):
    k, n = w.shape
    w = f64(np.asarray(w, np.float32).astype(ml_dtypes.bfloat16)).reshape(k // 32, 32, n)
    amax = np.abs(w).max(1)
    if fmt == "e4m3":
        byte = np.frexp(amax)[1] - 1 + 127 - 7
    else:
        mant, ex = np.frexp(amax / 6.0)
        byte = np.where(mant > 0.5, ex, ex - 1) + 127
    byte = np.clip(np.where(amax > 0, byte, 1), 1, 254)
    scaled = (w * np.exp2(127.0 - byte)[:, None, :]).reshape(k, n).astype(np.float32)
    by_word = np.ascontiguousarray(scaled.reshape(k // 512, 128, 4, n).transpose(0, 1, 3, 2))
    if fmt == "e4m3":
        words = by_word.astype(ml_dtypes.float8_e4m3fn).view(np.uint8)
    else:
        c = by_word.astype(ml_dtypes.float4_e2m1fn).view(np.uint8) & 0xF
        words = (c[..., 0::2] | (c[..., 1::2] << 4)).reshape(k // 512, 128, 2 * n)
    return np.ascontiguousarray(words), np.ascontiguousarray(byte.astype(np.uint8).reshape(k // 512, 16, n))


def unpack_weight(words, scales, fmt):
    g, _, n = scales.shape
    words = np.ascontiguousarray(words).reshape(g, 128, n, -1)
    if fmt == "e4m3":
        vals = words.view(ml_dtypes.float8_e4m3fn).astype(np.float64)
    else:
        nib = np.empty((g, 128, n, 4), np.uint8)
        nib[..., 0::2] = words & 0xF
        nib[..., 1::2] = words >> 4
        vals = E2M1[nib]
    vals = vals * np.repeat(np.exp2(scales.astype(np.float64) - 127.0), 8, axis=1)[..., None]
    return vals.transpose(0, 1, 3, 2).reshape(g * 512, n)


D, T, I, Q, E, Z, M = 512, 2048, 512, 256, 512, 1024, 1024


def setup_inputs():
    n = np.random.standard_normal
    idx = np.random.permutation(T)[:I]
    idx2 = np.random.permutation(Z)[:I]
    idx3 = np.random.permutation(M)[:Q]
    fd = mx_kscale(D)
    fi = mx_kscale(I)
    ti = np.ones(T)
    ti[idx] = fi
    keysp = pack_weight(n((D, T)) / fd[:, None], "e2m1")
    return {
        "query": (n((D, Q)) * 1.0 / np.sqrt(D) * fd[:, None]).astype(np.float32),
        "query2": (n((D, Q)) * 1.0 / np.sqrt(D) * fd[:, None]).astype(np.float32),
        "keys_words": keysp[0],
        "keys_scales": keysp[1],
        "pages": (n((D, Z)) / fd[:, None]).astype(np.float32),
        "os": (np.random.uniform(0.02, 0.08, (1, I)) * fi).astype(np.float32),
        "vals": (n((E, T)) / ti).astype(np.float32),
        "old": (n((E, M)) * 2.0).astype(np.float32),
        "fade": (np.random.uniform(0.3, 0.9, (1, M))).astype(np.float32),
        "offs": striped(idx),
        "offs2": striped(idx2),
        "offs3": striped(idx3),
    }


def reference(query, query2, keys_words, keys_scales, pages, os, vals, old, fade, offs, offs2, offs3):
    idx = unstriped(offs)
    idx2 = unstriped(offs2)
    idx3 = unstriped(offs3)
    keysu = unpack_weight(keys_words, keys_scales, "e2m1")
    queryq = mxq(f64(query), 0, "e4m3")
    keysidxg = keysu[:, idx]
    a = queryq.T @ keysidxg
    query2q = mxq(f64(query2), 0, "e4m3")
    pagesq = mxq(f64(pages), 0, "e4m3")
    h0 = query2q.T @ pagesq
    s = np.maximum(a, h0[:, idx2])
    w = np.maximum(s, 0.0)
    wo1 = w * f64(os)
    wt1 = wo1.T
    vt1 = f64(vals)[:, idx].T
    vt1q = mxq(vt1, 0, "e4m3")
    wt1q = mxq(wt1, 0, "e4m3")
    o = vt1q.T @ wt1q
    of = np.zeros((E, M))
    of[:, idx3] = o
    y = f64(old) * f64(fade) + of
    return y

@@ -1,0 +1,271 @@
+from contextlib import ExitStack
+
+import concourse.mybir as mybir
+from concourse.masks import make_identity
+
+D, T, I, Q, E, Z, M = 512, 2048, 512, 256, 512, 1024, 1024
+FLOPS = 2 * (D * Q * I + D * Q * Z + I * E * Q)
+
+F32 = mybir.dt.float32
+BF16 = mybir.dt.bfloat16
+I32 = mybir.dt.int32
+U32 = mybir.dt.uint32
+U16 = mybir.dt.uint16
+U8 = mybir.dt.uint8
+FP8X4 = mybir.dt.float8_e4m3fn_x4
+FP4X4 = mybir.dt.float4_e2m1fn_x4
+ALU = mybir.AluOpType
+COPY = mybir.ActivationFunctionType.Copy
+
+P = 128
+PACK = 4
+BANK = 512
+PIECES = ((0, 512, 320), (512, 256, 0), (768, 256, 256))
+
+
+def tile_attend_widelarger_written_lean_kernel(
+    tc, query, query2, keys_words, keys_scales, pages, slot_factor, vals, old, fade, offs, offs2, offs3, out
+):
+    nc = tc.nc
+    with ExitStack() as ctx:
+        sb = ctx.enter_context(tc.tile_pool(name="sb", bufs=1))
+        ps = ctx.enter_context(tc.psum_pool(name="ps", bufs=1))
+
+        def tile(shape, dtype, name, tag=None):
+            return sb.tile(shape, dtype, name=name, tag=tag or name, align_bytes=64)
+
+        def bank(shape, name, number):
+            return ps.tile(shape, F32, name=name, tag=f"bank{number}")
+
+        def rows_by_four(x):
+            return x.rearrange("(p j) w -> p j w", j=PACK)
+
+        def interleave(engine, dst, src):
+            src = src.rearrange("p t c -> p c t")
+            if engine == "vector":
+                nc.vector.tensor_copy(dst, src)
+            else:
+                nc.scalar.activation(dst, src, COPY)
+
+        def quantize(grouped, width, name, tag=None):
+            codes = tile([P, width], U32, name + "_codes", tag)
+            scales = tile([P, width], U8, name + "_scales")
+            nc.vector.quantize_mx(
+                out=codes[:].bitcast(FP8X4), scales=scales[:], in_=grouped[:].rearrange("p w t -> p (w t)")
+            )
+            return codes, scales
+
+        def gather(engine, dst, window, offsets):
+            if engine == "vector":
+                nc.vector.tensor_copy(dst, window[:].indirect(offsets))
+            else:
+                nc.scalar.activation(dst, window[:].indirect(offsets), COPY)
+
+        def product(acc, left, left_cols, right, right_dtype):
+            nc.tensor.matmul_mx(
+                out=acc,
+                lhsT=left[0][:, left_cols].bitcast(FP8X4),
+                lhsT_scale=left[1][:, left_cols],
+                rhs=right[0][:].bitcast(right_dtype),
+                rhs_scale=right[1][:],
+                start=True,
+                stop=True,
+            )
+
+        halves = [slice(0, P), slice(P, 2 * P)]
+
+        list1 = tile([P, I // 16], U16, "list1")
+        list2 = tile([P, I // 16], U16, "list2")
+        list3 = tile([P, Q // 16], U16, "list3")
+        key_words = tile([P, T], U16, "key_words")
+        key_rows = tile([P, T // 4], I32, "key_rows")
+        key_bytes = tile([P, T], U8, "key_bytes")
+        q1_raw = tile([P, PACK, Q], F32, "q1_raw")
+        q2_raw = tile([P, PACK, Q], F32, "q2_raw")
+        page_raw = [tile([P, PACK, width], F32, f"page_raw{n}") for n, (first, width, share) in enumerate(PIECES)]
+        val_raw = [tile([P, T], F32, f"val_raw{b}") for b in range(4)]
+        old_raw = [tile([P, M], F32, f"old_raw{b}") for b in range(4)]
+        factor = tile([P, PACK], F32, "factor")
+        fade_col = tile([P, 2, 4], F32, "fade_col")
+        placed = [tile([P, M], F32, f"placed{b}") for b in range(3)]
+        ident = tile([P, P], F32, "ident")
+
+        nc.vector.memset(key_bytes[:].bitcast(I32), 0)
+        make_identity(nc, ident[:])
+        for window in placed:
+            nc.gpsimd.memset(window[:].bitcast(I32), 0)
+
+        def load_vals(b):
+            nc.sync.dma_start(val_raw[b][:], vals[b * P : (b + 1) * P, :])
+
+        def load_old(b):
+            nc.sync.dma_start(old_raw[b][:], old[b * P : (b + 1) * P, :])
+
+        def load_pages(n):
+            first, width, share = PIECES[n]
+            nc.sync.dma_start(page_raw[n][:], rows_by_four(pages)[:, :, first : first + width])
+
+        for r in range(4):
+            nc.sync.dma_start(key_rows[r:P:32, :], keys_scales[0].bitcast(I32)[r:16:4, :])
+        nc.sync.dma_start(list1[:], offs)
+        nc.sync.dma_start(key_words[:].bitcast(I32), keys_words[0].bitcast(I32))
+        nc.sync.dma_start(q2_raw[:], rows_by_four(query2))
+        for n in range(len(PIECES)):
+            load_pages(n)
+        nc.sync.dma_start(q1_raw[:], rows_by_four(query))
+        nc.sync.dma_start(list2[:], offs2)
+        nc.sync.dma_start(factor[:], slot_factor.rearrange("o (p t) -> p (o t)", t=PACK))
+        load_vals(0)
+        nc.sync.dma_start(fade_col[:], fade.rearrange("o (h p c) -> p (o h) c", h=2, c=4))
+        nc.sync.dma_start(list3[:], offs3)
+        load_vals(1)
+        load_old(0)
+        load_vals(2)
+        load_vals(3)
+        load_old(1)
+        load_old(2)
+        load_old(3)
+
+        for quadrant in range(4):
+            rows = slice(32 * quadrant, 32 * quadrant + 4)
+            nc.vector.tensor_copy(key_bytes[:].bitcast(I32)[rows, :], key_rows[rows, :])
+        key_words_g = tile([P, I], U16, "key_words_g")
+        key_bytes_g = tile([P, I], U8, "key_bytes_g")
+        gather("vector", key_bytes_g[:], key_bytes, list1[:])
+        gather("vector", key_words_g[:], key_words, list1[:])
+
+        q2_bf = tile([P, Q, PACK], BF16, "q2_bf")
+        interleave("scalar", q2_bf[:], q2_raw[:])
+        q2 = quantize(q2_bf, Q, "q2")
+        h0 = [tile([P, Z], F32, f"h0_{g}") for g in range(2)]
+        page_bf = []
+        for n, (first, width, share) in enumerate(PIECES):
+            page_bf.append(tile([P, width, PACK], BF16, f"page_bf{n}"))
+            if share > 0:
+                interleave("vector", page_bf[n][:, :share, :], page_raw[n][:, :, :share])
+            if share < width:
+                interleave("scalar", page_bf[n][:, share:, :], page_raw[n][:, :, share:])
+        for n, (first, width, share) in enumerate(PIECES):
+            page = quantize(page_bf[n], width, f"page{n}")
+            if width == BANK:
+                acc = [bank([P, BANK], f"h0_acc{n}{g}", (0, 4, 5)[n] + g)[:] for g in range(2)]
+            else:
+                both = bank([P, 2, width], f"h0_acc{n}", (0, 4, 5)[n])
+                acc = [both[:, g, :] for g in range(2)]
+            for g in range(2):
+                product(acc[g], q2, halves[g], page, FP8X4)
+            for g in range(2):
+                nc.scalar.copy(h0[g][:, first : first + width], acc[g])
+        q1_bf = tile([P, Q, PACK], BF16, "q1_bf")
+        interleave("vector", q1_bf[:], q1_raw[:])
+        q1 = quantize(q1_bf, Q, "q1")
+
+        scores = [bank([P, I], f"a_acc{g}", 2 + g) for g in range(2)]
+        for g in range(2):
+            product(scores[g][:], q1, halves[g], (key_words_g, key_bytes_g), FP4X4)
+        h0_g = [tile([P, I], F32, f"h0_g{g}") for g in range(2)]
+        gather("vector", h0_g[0][:, 0 : 512], h0[0], list2[:, 0 : 32])
+        gather("vector", h0_g[1][:, 0 : 512], h0[1], list2[:, 0 : 32])
+        turned = []
+        for g in range(2):
+            w = tile([P, PACK, P], F32, f"w{g}")
+            nc.vector.scalar_tensor_tensor(
+                out=w[:].rearrange("p t s -> p s t"),
+                in0=h0_g[g][:].rearrange("p (s t) -> p s t", t=PACK),
+                scalar=0.0,
+                in1=scores[g][:].rearrange("p (s t) -> p s t", t=PACK),
+                op0=ALU.max,
+                op1=ALU.max,
+            )
+            wt = bank([P, PACK, P], f"wt{g}", g)
+            for t in range(PACK):
+                nc.tensor.transpose(wt[:, t, :], w[:, t, :], ident[:])
+            turned.append(wt)
+        w_bf = [tile([P, P, PACK], BF16, f"w_bf{g}") for g in range(2)]
+        for g in range(2):
+            nc.vector.tensor_tensor(
+                out=w_bf[g][:],
+                in0=turned[g][:].rearrange("p t q -> p q t"),
+                in1=factor[:].unsqueeze(1).to_broadcast([P, P, PACK]),
+                op=ALU.mult,
+            )
+        w_codes = tile([P, Q], U32, "w_codes")
+        w_scales = tile([P, Q], U8, "w_scales")
+        for g in range(2):
+            nc.vector.quantize_mx(
+                out=w_codes[:, halves[g]].bitcast(FP8X4),
+                scales=w_scales[:, halves[g]],
+                in_=w_bf[g][:].rearrange("p q t -> p (q t)"),
+            )
+
+        fade_all = []
+        for h in range(2):
+            spread = bank([P, 4, P], f"fade_all{h}", 6 + h)
+            for c in range(4):
+                nc.tensor.transpose(spread[:, c, :], fade_col[:, h, c : c + 1].to_broadcast([P, P]), ident[:])
+            fade_all.append(spread)
+
+        v_ops = {}
+        faded = {}
+
+        def values(b):
+            picked = tile([P, I], BF16, f"picked{b}", [None, None, "w_bf1", None][b])
+            gather(["scalar","scalar","vector","vector"][b], picked[:], val_raw[b], list1[:])
+            words = picked[:].bitcast(F32)
+            vt = bank([P, 2, P], f"vt{b}", (4, 5, 0, 1)[b])
+            for u in range(2):
+                nc.tensor.transpose(vt[:, u, :], words[:, u::2], ident[:])
+            v_bf = tile([P, P, PACK], BF16, f"v_bf{b}")
+            (nc.vector.tensor_copy if ["scalar","scalar","vector","vector"][b] == "vector" else nc.scalar.copy)(
+                v_bf[:].rearrange("p e t -> p (e t)").bitcast(F32).rearrange("p (e u) -> p e u", u=2),
+                vt[:].rearrange("p u e -> p e u"),
+            )
+            v_ops[b] = quantize(v_bf, P, f"v{b}", [None, "w_bf0", None, None][b])
+
+        def fade_old(b):
+            faded[b] = tile([P, M], F32, f"faded{b}", ["val_raw2", "val_raw3", "picked3", "v_bf3"][b])
+            for h in range(2):
+                cols = slice(h * BANK, (h + 1) * BANK)
+                nc.vector.tensor_tensor(
+                    out=faded[b][:, cols].rearrange("p (n c) -> p n c", c=4),
+                    in0=old_raw[b][:, cols].rearrange("p (n c) -> p n c", c=4),
+                    in1=fade_all[h][:].rearrange("p c n -> p n c"),
+                    op=ALU.mult,
+                )
+
+        def place(b):
+            acc = bank([P, Q], f"o_acc{b}", (5, 2, 3, 4)[b])
+            product(acc[:], v_ops[b], slice(0, P), (w_codes, w_scales), FP8X4)
+            o = tile([P, Q], F32, f"o{b}", [None, None, None, None][b])
+            nc.scalar.copy(o[:], acc[:])
+            window = placed[b % len(placed)]
+            if ["scalar","scalar","scalar","scalar"][b] == "vector":
+                nc.vector.tensor_copy(window[:].indirect(list3[:]), o[:])
+            else:
+                nc.scalar.activation(window[:].indirect(list3[:]), o[:], COPY)
+
+        def finish(b):
+            y = tile([P, M], F32, f"y{b}", [None, None, None, None][b])
+            window = placed[b % len(placed)]
+            for h in range(2):
+                cols = slice(h * BANK, (h + 1) * BANK)
+                engine = nc.vector if "ggggggvv"[2 * b + h] == "v" else nc.gpsimd
+                engine.tensor_tensor(out=y[:, cols], in0=faded[b][:, cols], in1=window[:, cols], op=ALU.add)
+                nc.sync.dma_start(out[b * P : (b + 1) * P, cols], y[:, cols])
+
+        values(0)
+        values(1)
+        place(0)
+        place(1)
+        values(2)
+        values(3)
+        place(2)
+        fade_old(0)
+        finish(0)
+        place(3)
+        fade_old(1)
+        finish(1)
+        fade_old(2)
+        finish(2)
+        fade_old(3)
+        finish(3)

@@ -41,7 +41,8 @@ def tile_attend_widelarger_written_lean_kernel(
             return x.rearrange("(p j) w -> p j w", j=PACK)
 
         def interleave(engine, dst, src):
-            src = src.rearrange("p t c -> p c t")
+            dst = dst.rearrange("p (c i) t -> p c t i", i=4)
+            src = src.rearrange("p t (c i) -> p c t i", i=4)
             if engine == "vector":
                 nc.vector.tensor_copy(dst, src)
             else:
@@ -87,13 +88,13 @@ def tile_attend_widelarger_written_lean_kernel(
         old_raw = [tile([P, M], F32, f"old_raw{b}") for b in range(4)]
         factor = tile([P, PACK], F32, "factor")
         fade_col = tile([P, 2, 4], F32, "fade_col")
-        placed = [tile([P, M], F32, f"placed{b}") for b in range(3)]
+        placed = [tile([P, M], F32, f"placed{b}") for b in range(2)]
         ident = tile([P, P], F32, "ident")
 
         nc.vector.memset(key_bytes[:].bitcast(I32), 0)
         make_identity(nc, ident[:])
         for window in placed:
-            nc.gpsimd.memset(window[:].bitcast(I32), 0)
+            nc.vector.memset(window[:].bitcast(I32), 0)
 
         def load_vals(b):
             nc.sync.dma_start(val_raw[b][:], vals[b * P : (b + 1) * P, :])
@@ -121,8 +122,8 @@ def tile_attend_widelarger_written_lean_kernel(
         load_vals(1)
         load_old(0)
         load_vals(2)
-        load_vals(3)
         load_old(1)
+        load_vals(3)
         load_old(2)
         load_old(3)
 
@@ -206,24 +207,28 @@ def tile_attend_widelarger_written_lean_kernel(
             fade_all.append(spread)
 
         v_ops = {}
+        v_bfs = {}
         faded = {}
 
-        def values(b):
-            picked = tile([P, I], BF16, f"picked{b}", [None, None, "w_bf1", None][b])
-            gather(["scalar","scalar","vector","vector"][b], picked[:], val_raw[b], list1[:])
+        def pick(b):
+            picked = tile([P, I], BF16, f"picked{b}", [None, None, None, None][b])
+            gather(["scalar","scalar","scalar","vector"][b], picked[:], val_raw[b], list1[:])
             words = picked[:].bitcast(F32)
             vt = bank([P, 2, P], f"vt{b}", (4, 5, 0, 1)[b])
             for u in range(2):
                 nc.tensor.transpose(vt[:, u, :], words[:, u::2], ident[:])
             v_bf = tile([P, P, PACK], BF16, f"v_bf{b}")
-            (nc.vector.tensor_copy if ["scalar","scalar","vector","vector"][b] == "vector" else nc.scalar.copy)(
+            (nc.vector.tensor_copy if ["scalar","scalar","scalar","scalar"][b] == "vector" else nc.scalar.copy)(
                 v_bf[:].rearrange("p e t -> p (e t)").bitcast(F32).rearrange("p (e u) -> p e u", u=2),
                 vt[:].rearrange("p u e -> p e u"),
             )
-            v_ops[b] = quantize(v_bf, P, f"v{b}", [None, "w_bf0", None, None][b])
+            v_bfs[b] = v_bf
+
+        def quant(b):
+            v_ops[b] = quantize(v_bfs[b], P, f"v{b}", [None, "w_bf0", None, "old_raw2"][b])
 
         def fade_old(b):
-            faded[b] = tile([P, M], F32, f"faded{b}", ["val_raw2", "val_raw3", "picked3", "v_bf3"][b])
+            faded[b] = tile([P, M], F32, f"faded{b}", ["w_bf1", None, None, None][b])
             for h in range(2):
                 cols = slice(h * BANK, (h + 1) * BANK)
                 nc.vector.tensor_tensor(
@@ -234,9 +239,9 @@ def tile_attend_widelarger_written_lean_kernel(
                 )
 
         def place(b):
-            acc = bank([P, Q], f"o_acc{b}", (5, 2, 3, 4)[b])
+            acc = bank([P, Q], f"o_acc{b}", (5, 2, 1, 4)[b])
             product(acc[:], v_ops[b], slice(0, P), (w_codes, w_scales), FP8X4)
-            o = tile([P, Q], F32, f"o{b}", [None, None, None, None][b])
+            o = tile([P, Q], F32, f"o{b}", ["val_raw2", None, None, None][b])
             nc.scalar.copy(o[:], acc[:])
             window = placed[b % len(placed)]
             if ["scalar","scalar","scalar","scalar"][b] == "vector":
@@ -245,27 +250,31 @@ def tile_attend_widelarger_written_lean_kernel(
                 nc.scalar.activation(window[:].indirect(list3[:]), o[:], COPY)
 
         def finish(b):
-            y = tile([P, M], F32, f"y{b}", [None, None, None, None][b])
+            y = tile([P, M], F32, f"y{b}", ["val_raw3", None, None, None][b])
             window = placed[b % len(placed)]
-            for h in range(2):
-                cols = slice(h * BANK, (h + 1) * BANK)
-                engine = nc.vector if "ggggggvv"[2 * b + h] == "v" else nc.gpsimd
-                engine.tensor_tensor(out=y[:, cols], in0=faded[b][:, cols], in1=window[:, cols], op=ALU.add)
+            parts = (1, 1, 1, 2)[b]
+            for h in range(parts):
+                cols = slice(h * M // parts, (h + 1) * M // parts)
+                nc.vector.tensor_tensor(out=y[:, cols], in0=faded[b][:, cols], in1=window[:, cols], op=ALU.add)
                 nc.sync.dma_start(out[b * P : (b + 1) * P, cols], y[:, cols])
 
-        values(0)
-        values(1)
+        pick(0)
+        quant(0)
+        pick(1)
+        quant(1)
+        pick(2)
         place(0)
-        place(1)
-        values(2)
-        values(3)
-        place(2)
         fade_old(0)
-        finish(0)
-        place(3)
+        quant(2)
         fade_old(1)
-        finish(1)
+        pick(3)
+        place(1)
+        finish(0)
         fade_old(2)
-        finish(2)
+        quant(3)
+        place(2)
+        finish(1)
         fade_old(3)
+        place(3)
+        finish(2)
         finish(3)

@@ -88,7 +88,7 @@ def tile_attend_widelarger_written_lean_kernel(
         old_raw = [tile([P, M], F32, f"old_raw{b}") for b in range(4)]
         factor = tile([P, PACK], F32, "factor")
         fade_col = tile([P, 2, 4], F32, "fade_col")
-        placed = [tile([P, M], F32, f"placed{b}") for b in range(2)]
+        placed = [tile([P, M], F32, f"placed{b}") for b in range(3)]
         ident = tile([P, P], F32, "ident")
 
         nc.vector.memset(key_bytes[:].bitcast(I32), 0)
@@ -111,13 +111,14 @@ def tile_attend_widelarger_written_lean_kernel(
         nc.sync.dma_start(list1[:], offs)
         nc.sync.dma_start(key_words[:].bitcast(I32), keys_words[0].bitcast(I32))
         nc.sync.dma_start(q2_raw[:], rows_by_four(query2))
-        for n in range(len(PIECES)):
+        load_pages(0)
+        nc.sync.dma_start(fade_col[:], fade.rearrange("o (h p c) -> p (o h) c", h=2, c=4))
+        for n in range(1, len(PIECES)):
             load_pages(n)
         nc.sync.dma_start(q1_raw[:], rows_by_four(query))
         nc.sync.dma_start(list2[:], offs2)
         nc.sync.dma_start(factor[:], slot_factor.rearrange("o (p t) -> p (o t)", t=PACK))
         load_vals(0)
-        nc.sync.dma_start(fade_col[:], fade.rearrange("o (h p c) -> p (o h) c", h=2, c=4))
         nc.sync.dma_start(list3[:], offs3)
         load_vals(1)
         load_old(0)
@@ -164,6 +165,25 @@ def tile_attend_widelarger_written_lean_kernel(
         scores = [bank([P, I], f"a_acc{g}", 2 + g) for g in range(2)]
         for g in range(2):
             product(scores[g][:], q1, halves[g], (key_words_g, key_bytes_g), FP4X4)
+        v_ops = {}
+        v_bfs = {}
+        faded = {}
+
+        def pick(b):
+            picked = tile([P, I], BF16, f"picked{b}", [None, None, None, None][b])
+            gather(["scalar","scalar","scalar","vector"][b], picked[:], val_raw[b], list1[:])
+            words = picked[:].bitcast(F32)
+            vt = bank([P, 2, P], f"vt{b}", (4, 5, 0, 1)[b])
+            for u in range(2):
+                nc.tensor.transpose(vt[:, u, :], words[:, u::2], ident[:])
+            v_bf = tile([P, P, PACK], BF16, f"v_bf{b}")
+            (nc.vector.tensor_copy if ["scalar","scalar","vector","vector"][b] == "vector" else nc.scalar.copy)(
+                v_bf[:].rearrange("p e t -> p (e t)").bitcast(F32).rearrange("p (e u) -> p e u", u=2),
+                vt[:].rearrange("p u e -> p e u"),
+            )
+            v_bfs[b] = v_bf
+
+        pick(0)
         h0_g = [tile([P, I], F32, f"h0_g{g}") for g in range(2)]
         gather("vector", h0_g[0][:, 0 : 512], h0[0], list2[:, 0 : 32])
         gather("vector", h0_g[1][:, 0 : 512], h0[1], list2[:, 0 : 32])
@@ -206,26 +226,8 @@ def tile_attend_widelarger_written_lean_kernel(
                 nc.tensor.transpose(spread[:, c, :], fade_col[:, h, c : c + 1].to_broadcast([P, P]), ident[:])
             fade_all.append(spread)
 
-        v_ops = {}
-        v_bfs = {}
-        faded = {}
-
-        def pick(b):
-            picked = tile([P, I], BF16, f"picked{b}", [None, None, None, None][b])
-            gather(["scalar","scalar","scalar","vector"][b], picked[:], val_raw[b], list1[:])
-            words = picked[:].bitcast(F32)
-            vt = bank([P, 2, P], f"vt{b}", (4, 5, 0, 1)[b])
-            for u in range(2):
-                nc.tensor.transpose(vt[:, u, :], words[:, u::2], ident[:])
-            v_bf = tile([P, P, PACK], BF16, f"v_bf{b}")
-            (nc.vector.tensor_copy if ["scalar","scalar","scalar","scalar"][b] == "vector" else nc.scalar.copy)(
-                v_bf[:].rearrange("p e t -> p (e t)").bitcast(F32).rearrange("p (e u) -> p e u", u=2),
-                vt[:].rearrange("p u e -> p e u"),
-            )
-            v_bfs[b] = v_bf
-
         def quant(b):
-            v_ops[b] = quantize(v_bfs[b], P, f"v{b}", [None, "w_bf0", None, "old_raw2"][b])
+            v_ops[b] = quantize(v_bfs[b], P, f"v{b}", [None, "w_bf0", None, None][b])
 
         def fade_old(b):
             faded[b] = tile([P, M], F32, f"faded{b}", ["w_bf1", None, None, None][b])
@@ -238,19 +240,17 @@ def tile_attend_widelarger_written_lean_kernel(
                     op=ALU.mult,
                 )
 
-        def place(b):
-            acc = bank([P, Q], f"o_acc{b}", (5, 2, 1, 4)[b])
-            product(acc[:], v_ops[b], slice(0, P), (w_codes, w_scales), FP8X4)
-            o = tile([P, Q], F32, f"o{b}", ["val_raw2", None, None, None][b])
+        def place(blocks, number, tag=None):
+            acc = bank([P, len(blocks), Q], f"o_acc{blocks[0]}", number)
+            for n, b in enumerate(blocks):
+                product(acc[:, n, :], v_ops[b], slice(0, P), (w_codes, w_scales), FP8X4)
+            o = tile([P, len(blocks), Q], F32, f"o{blocks[0]}", tag)
             nc.scalar.copy(o[:], acc[:])
-            window = placed[b % len(placed)]
-            if ["scalar","scalar","scalar","scalar"][b] == "vector":
-                nc.vector.tensor_copy(window[:].indirect(list3[:]), o[:])
-            else:
-                nc.scalar.activation(window[:].indirect(list3[:]), o[:], COPY)
+            for n, b in enumerate(blocks):
+                nc.scalar.activation(placed[b % len(placed)][:].indirect(list3[:]), o[:, n, :], COPY)
 
         def finish(b):
-            y = tile([P, M], F32, f"y{b}", ["val_raw3", None, None, None][b])
+            y = tile([P, M], F32, f"y{b}", ["val_raw3", "v_bf3", None, None][b])
             window = placed[b % len(placed)]
             parts = (1, 1, 1, 2)[b]
             for h in range(parts):
@@ -258,23 +258,21 @@ def tile_attend_widelarger_written_lean_kernel(
                 nc.vector.tensor_tensor(out=y[:, cols], in0=faded[b][:, cols], in1=window[:, cols], op=ALU.add)
                 nc.sync.dma_start(out[b * P : (b + 1) * P, cols], y[:, cols])
 
-        pick(0)
         quant(0)
         pick(1)
         quant(1)
         pick(2)
-        place(0)
+        place((0, 1), 2, "val_raw2")
         fade_old(0)
         quant(2)
         fade_old(1)
         pick(3)
-        place(1)
+        place((2,), 3)
         finish(0)
-        fade_old(2)
         quant(3)
-        place(2)
+        fade_old(2)
+        place((3,), 4)
         finish(1)
         fade_old(3)
-        place(3)
         finish(2)
         finish(3)

from contextlib import ExitStack

import concourse.mybir as mybir
from concourse.masks import make_identity

D, T, I, Q, E, Z, M = 512, 2048, 512, 256, 512, 1024, 1024
FLOPS = 2 * (D * Q * I + D * Q * Z + I * E * Q)

F32 = mybir.dt.float32
BF16 = mybir.dt.bfloat16
I32 = mybir.dt.int32
U32 = mybir.dt.uint32
U16 = mybir.dt.uint16
U8 = mybir.dt.uint8
FP8X4 = mybir.dt.float8_e4m3fn_x4
FP4X4 = mybir.dt.float4_e2m1fn_x4
ALU = mybir.AluOpType
COPY = mybir.ActivationFunctionType.Copy

P = 128
PACK = 4
BANK = 512
PIECES = ((0, 512, 320), (512, 256, 0), (768, 256, 256))


def tile_attend_widelarger_written_lean_kernel(
    tc, query, query2, keys_words, keys_scales, pages, slot_factor, vals, old, fade, offs, offs2, offs3, out
):
    nc = tc.nc
    with ExitStack() as ctx:
        sb = ctx.enter_context(tc.tile_pool(name="sb", bufs=1))
        ps = ctx.enter_context(tc.psum_pool(name="ps", bufs=1))

        def tile(shape, dtype, name, tag=None):
            return sb.tile(shape, dtype, name=name, tag=tag or name, align_bytes=64)

        def bank(shape, name, number):
            return ps.tile(shape, F32, name=name, tag=f"bank{number}")

        def rows_by_four(x):
            return x.rearrange("(p j) w -> p j w", j=PACK)

        def interleave(engine, dst, src):
            dst = dst.rearrange("p (c i) t -> p c t i", i=4)
            src = src.rearrange("p t (c i) -> p c t i", i=4)
            if engine == "vector":
                nc.vector.tensor_copy(dst, src)
            else:
                nc.scalar.activation(dst, src, COPY)

        def quantize(grouped, width, name, tag=None):
            codes = tile([P, width], U32, name + "_codes", tag)
            scales = tile([P, width], U8, name + "_scales")
            nc.vector.quantize_mx(
                out=codes[:].bitcast(FP8X4), scales=scales[:], in_=grouped[:].rearrange("p w t -> p (w t)")
            )
            return codes, scales

        def gather(engine, dst, window, offsets):
            if engine == "vector":
                nc.vector.tensor_copy(dst, window[:].indirect(offsets))
            else:
                nc.scalar.activation(dst, window[:].indirect(offsets), COPY)

        def product(acc, left, left_cols, right, right_dtype):
            nc.tensor.matmul_mx(
                out=acc,
                lhsT=left[0][:, left_cols].bitcast(FP8X4),
                lhsT_scale=left[1][:, left_cols],
                rhs=right[0][:].bitcast(right_dtype),
                rhs_scale=right[1][:],
                start=True,
                stop=True,
            )

        halves = [slice(0, P), slice(P, 2 * P)]

        list1 = tile([P, I // 16], U16, "list1")
        list2 = tile([P, I // 16], U16, "list2")
        list3 = tile([P, Q // 16], U16, "list3")
        key_words = tile([P, T], U16, "key_words")
        key_rows = tile([P, T // 4], I32, "key_rows")
        key_bytes = tile([P, T], U8, "key_bytes")
        q1_raw = tile([P, PACK, Q], F32, "q1_raw")
        q2_raw = tile([P, PACK, Q], F32, "q2_raw")
        page_raw = [tile([P, PACK, width], F32, f"page_raw{n}") for n, (first, width, share) in enumerate(PIECES)]
        val_raw = [tile([P, T], F32, f"val_raw{b}") for b in range(4)]
        old_raw = [tile([P, M], F32, f"old_raw{b}") for b in range(4)]
        factor = tile([P, PACK], F32, "factor")
        fade_col = tile([P, 2, 4], F32, "fade_col")
        placed = [tile([P, M], F32, f"placed{b}") for b in range(3)]
        ident = tile([P, P], F32, "ident")

        nc.vector.memset(key_bytes[:].bitcast(I32), 0)
        make_identity(nc, ident[:])
        for window in placed:
            nc.vector.memset(window[:].bitcast(I32), 0)

        def load_vals(b):
            nc.sync.dma_start(val_raw[b][:], vals[b * P : (b + 1) * P, :])

        def load_old(b):
            nc.sync.dma_start(old_raw[b][:], old[b * P : (b + 1) * P, :])

        def load_pages(n):
            first, width, share = PIECES[n]
            nc.sync.dma_start(page_raw[n][:], rows_by_four(pages)[:, :, first : first + width])

        for r in range(4):
            nc.sync.dma_start(key_rows[r:P:32, :], keys_scales[0].bitcast(I32)[r:16:4, :])
        nc.sync.dma_start(list1[:], offs)
        nc.sync.dma_start(key_words[:].bitcast(I32), keys_words[0].bitcast(I32))
        nc.sync.dma_start(q2_raw[:], rows_by_four(query2))
        load_pages(0)
        nc.sync.dma_start(fade_col[:], fade.rearrange("o (h p c) -> p (o h) c", h=2, c=4))
        for n in range(1, len(PIECES)):
            load_pages(n)
        nc.sync.dma_start(q1_raw[:], rows_by_four(query))
        nc.sync.dma_start(list2[:], offs2)
        nc.sync.dma_start(factor[:], slot_factor.rearrange("o (p t) -> p (o t)", t=PACK))
        load_vals(0)
        nc.sync.dma_start(list3[:], offs3)
        load_vals(1)
        load_old(0)
        load_vals(2)
        load_old(1)
        load_vals(3)
        load_old(2)
        load_old(3)

        for quadrant in range(4):
            rows = slice(32 * quadrant, 32 * quadrant + 4)
            nc.vector.tensor_copy(key_bytes[:].bitcast(I32)[rows, :], key_rows[rows, :])
        key_words_g = tile([P, I], U16, "key_words_g")
        key_bytes_g = tile([P, I], U8, "key_bytes_g")
        gather("vector", key_bytes_g[:], key_bytes, list1[:])
        gather("vector", key_words_g[:], key_words, list1[:])

        q2_bf = tile([P, Q, PACK], BF16, "q2_bf")
        interleave("scalar", q2_bf[:], q2_raw[:])
        q2 = quantize(q2_bf, Q, "q2")
        h0 = [tile([P, Z], F32, f"h0_{g}") for g in range(2)]
        page_bf = []
        for n, (first, width, share) in enumerate(PIECES):
            page_bf.append(tile([P, width, PACK], BF16, f"page_bf{n}"))
            if share > 0:
                interleave("vector", page_bf[n][:, :share, :], page_raw[n][:, :, :share])
            if share < width:
                interleave("scalar", page_bf[n][:, share:, :], page_raw[n][:, :, share:])
        for n, (first, width, share) in enumerate(PIECES):
            page = quantize(page_bf[n], width, f"page{n}")
            if width == BANK:
                acc = [bank([P, BANK], f"h0_acc{n}{g}", (0, 4, 5)[n] + g)[:] for g in range(2)]
            else:
                both = bank([P, 2, width], f"h0_acc{n}", (0, 4, 5)[n])
                acc = [both[:, g, :] for g in range(2)]
            for g in range(2):
                product(acc[g], q2, halves[g], page, FP8X4)
            for g in range(2):
                nc.scalar.copy(h0[g][:, first : first + width], acc[g])
        q1_bf = tile([P, Q, PACK], BF16, "q1_bf")
        interleave("vector", q1_bf[:], q1_raw[:])
        q1 = quantize(q1_bf, Q, "q1")

        scores = [bank([P, I], f"a_acc{g}", 2 + g) for g in range(2)]
        for g in range(2):
            product(scores[g][:], q1, halves[g], (key_words_g, key_bytes_g), FP4X4)
        v_ops = {}
        v_bfs = {}
        faded = {}

        def pick(b):
            picked = tile([P, I], BF16, f"picked{b}", [None, None, None, None][b])
            gather(["scalar","scalar","scalar","vector"][b], picked[:], val_raw[b], list1[:])
            words = picked[:].bitcast(F32)
            vt = bank([P, 2, P], f"vt{b}", (4, 5, 0, 1)[b])
            for u in range(2):
                nc.tensor.transpose(vt[:, u, :], words[:, u::2], ident[:])
            v_bf = tile([P, P, PACK], BF16, f"v_bf{b}")
            (nc.vector.tensor_copy if ["scalar","scalar","vector","vector"][b] == "vector" else nc.scalar.copy)(
                v_bf[:].rearrange("p e t -> p (e t)").bitcast(F32).rearrange("p (e u) -> p e u", u=2),
                vt[:].rearrange("p u e -> p e u"),
            )
            v_bfs[b] = v_bf

        pick(0)
        h0_g = [tile([P, I], F32, f"h0_g{g}") for g in range(2)]
        gather("vector", h0_g[0][:, 0 : 512], h0[0], list2[:, 0 : 32])
        gather("vector", h0_g[1][:, 0 : 512], h0[1], list2[:, 0 : 32])
        turned = []
        for g in range(2):
            w = tile([P, PACK, P], F32, f"w{g}")
            nc.vector.scalar_tensor_tensor(
                out=w[:].rearrange("p t s -> p s t"),
                in0=h0_g[g][:].rearrange("p (s t) -> p s t", t=PACK),
                scalar=0.0,
                in1=scores[g][:].rearrange("p (s t) -> p s t", t=PACK),
                op0=ALU.max,
                op1=ALU.max,
            )
            wt = bank([P, PACK, P], f"wt{g}", g)
            for t in range(PACK):
                nc.tensor.transpose(wt[:, t, :], w[:, t, :], ident[:])
            turned.append(wt)
        w_bf = [tile([P, P, PACK], BF16, f"w_bf{g}") for g in range(2)]
        for g in range(2):
            nc.vector.tensor_tensor(
                out=w_bf[g][:],
                in0=turned[g][:].rearrange("p t q -> p q t"),
                in1=factor[:].unsqueeze(1).to_broadcast([P, P, PACK]),
                op=ALU.mult,
            )
        w_codes = tile([P, Q], U32, "w_codes")
        w_scales = tile([P, Q], U8, "w_scales")
        for g in range(2):
            nc.vector.quantize_mx(
                out=w_codes[:, halves[g]].bitcast(FP8X4),
                scales=w_scales[:, halves[g]],
                in_=w_bf[g][:].rearrange("p q t -> p (q t)"),
            )

        fade_all = []
        for h in range(2):
            spread = bank([P, 4, P], f"fade_all{h}", 6 + h)
            for c in range(4):
                nc.tensor.transpose(spread[:, c, :], fade_col[:, h, c : c + 1].to_broadcast([P, P]), ident[:])
            fade_all.append(spread)

        def quant(b):
            v_ops[b] = quantize(v_bfs[b], P, f"v{b}", [None, "w_bf0", None, None][b])

        def fade_old(b):
            faded[b] = tile([P, M], F32, f"faded{b}", ["w_bf1", None, None, None][b])
            for h in range(2):
                cols = slice(h * BANK, (h + 1) * BANK)
                nc.vector.tensor_tensor(
                    out=faded[b][:, cols].rearrange("p (n c) -> p n c", c=4),
                    in0=old_raw[b][:, cols].rearrange("p (n c) -> p n c", c=4),
                    in1=fade_all[h][:].rearrange("p c n -> p n c"),
                    op=ALU.mult,
                )

        def place(blocks, number, tag=None):
            acc = bank([P, len(blocks), Q], f"o_acc{blocks[0]}", number)
            for n, b in enumerate(blocks):
                product(acc[:, n, :], v_ops[b], slice(0, P), (w_codes, w_scales), FP8X4)
            o = tile([P, len(blocks), Q], F32, f"o{blocks[0]}", tag)
            nc.scalar.copy(o[:], acc[:])
            for n, b in enumerate(blocks):
                nc.scalar.activation(placed[b % len(placed)][:].indirect(list3[:]), o[:, n, :], COPY)

        def finish(b):
            y = tile([P, M], F32, f"y{b}", ["val_raw3", "v_bf3", None, None][b])
            window = placed[b % len(placed)]
            parts = (1, 1, 1, 2)[b]
            for h in range(parts):
                cols = slice(h * M // parts, (h + 1) * M // parts)
                nc.vector.tensor_tensor(out=y[:, cols], in0=faded[b][:, cols], in1=window[:, cols], op=ALU.add)
                nc.sync.dma_start(out[b * P : (b + 1) * P, cols], y[:, cols])

        quant(0)
        pick(1)
        quant(1)
        pick(2)
        place((0, 1), 2, "val_raw2")
        fade_old(0)
        quant(2)
        fade_old(1)
        pick(3)
        place((2,), 3)
        finish(0)
        quant(3)
        fade_old(2)
        place((3,), 4)
        finish(1)
        fade_old(3)
        finish(2)
        finish(3)
